import numpy as np
CORES = [6,14,22,30,38,46,54,62,70,78,86,94,102,110,118,126]
N = 16
ROOT = 12
def setup_inputs(rng):
    return {"x": rng.standard_normal((N, 128, 1024), dtype=np.float32)}
def reference(x):
    y = np.full(x.shape, np.nan, x.dtype)
    y[ROOT] = x.sum(axis=0, dtype=np.float64).astype(x.dtype)
    return {"y": y}

@@ -1,0 +1,130 @@
+import concourse.bass as bass
+import comms_topo
+
+NCHIP = 16
+RANKCORE = 6
+ROOTRANK = 12
+OWNER = {0: 7, 1: 3}
+WIDTH = {0: 32, 1: 32}
+CHUNKS = {0: 1, 1: 1}
+SENDER = {("same", 0): 6, ("cross", 0): 6, ("cross", 1): 2, ("same", 1): 0}
+SEND_ORDER = [("cross", 1), ("same", 1), ("cross", 0), ("same", 0)]
+
+SCRATCH = {
+    "stage0": ("dram", [NCHIP * CHUNKS[0], 128, WIDTH[0]], "float32"),
+    "stage1": ("dram", [NCHIP * CHUNKS[1], 128, WIDTH[1]], "float32"),
+    "gat0": ("dram", [NCHIP * CHUNKS[0], 128, WIDTH[0]], "float32"),
+    "gat1": ("dram", [NCHIP * CHUNKS[1], 128, WIDTH[1]], "float32"),
+    "land0": ("dram", [NCHIP * CHUNKS[0], 128, WIDTH[0]], "float32"),
+    "land1": ("dram", [NCHIP * CHUNKS[1], 128, WIDTH[1]], "float32"),
+}
+SEMAPHORES = ["st", "sent",
+              "ld00", "ld01", "ld02", "ld03", "ld10", "ld11", "ld12", "ld13",
+              "hop0", "hop1", "hop2", "hop3", "arr0", "arr1", "arr2", "arr3",
+              "fin00", "fin01", "fin02", "fin03", "fin10", "fin11", "fin12", "fin13"]
+
+
+def dstid(c):
+    rid, pid, se = comms_topo.addr(c)
+    return bass.DstId(rid=rid, pnc=pid)
+
+
+def chips_of(par):
+    return [c for c in range(NCHIP) if (c & 1) == par]
+
+
+def rank_program(g, core, T, topo):
+    ch, k = divmod(core, 8)
+    par = ch & 1
+    root = T.cores[ROOTRANK]
+    S = T.sem
+    stage = {0: T.stage0, 1: T.stage1}
+    gat = {0: T.gat0, 1: T.gat1}
+    land = {0: T.land0, 1: T.land1}
+    ld = {0: [S.ld00, S.ld01, S.ld02, S.ld03], 1: [S.ld10, S.ld11, S.ld12, S.ld13]}
+    fin = {0: [S.fin00, S.fin01, S.fin02, S.fin03], 1: [S.fin10, S.fin11, S.fin12, S.fin13]}
+    hop = [S.hop0, S.hop1, S.hop2, S.hop3]
+    arr = [S.arr0, S.arr1, S.arr2, S.arr3]
+    maxc = max(CHUNKS.values())
+    sent = 0
+
+    def xrows(d, c):
+        r0 = (0 if d == 0 else 2 * WIDTH[0] * CHUNKS[0]) + 2 * WIDTH[d] * c
+        return r0, r0 + 2 * WIDTH[d]
+
+    def owner_par(rel):
+        return par if rel == "same" else 1 - par
+
+    def scatter(rel, d, c):
+        trs = [bass.RemoteDMATransfer(dst_ids=[dstid(oc * 8 + OWNER[d])], dma_engine_mask=1 << i,
+                                      remote_sem=arr[c], src=stage[d][c * NCHIP + oc], dst=gat[d][c * NCHIP + ch])
+               for i, oc in enumerate(chips_of(owner_par(rel)))]
+        g.remote_dma_fused(trs, local_sem=S.sent)
+        return len(trs)
+
+    hops = [key for key in SEND_ORDER if SENDER[key] != RANKCORE]
+    mine = [key for key in SEND_ORDER if SENDER[key] == k]
+    hop_ne = 16 // (8 * len(hops)) if len(hops) in (1, 2) else 1
+
+    if k == RANKCORE:
+        for c in range(maxc):
+            for d in (1, 0):
+                if c < CHUNKS[d]:
+                    r0, r1 = xrows(d, c)
+                    g.dma_start(stage[d][c * NCHIP:(c + 1) * NCHIP], T.x[r0:r1, :]).then_inc(ld[d][c], 16)
+        for c in range(maxc):
+            have = set()
+            trs = [(d, c * NCHIP + oc, ch * 8 + SENDER[(rel, d)])
+                   for rel, d in hops if c < CHUNKS[d] for oc in chips_of(owner_par(rel))]
+            for d in (1, 0):
+                if any(t[0] == d for t in trs):
+                    g.wait_ge(ld[d][c], 16)
+                    have.add(d)
+            for i0 in range(0, len(trs), 16):
+                blk = trs[i0:i0 + 16]
+                g.remote_dma_fused(
+                    [bass.RemoteDMATransfer(dst_ids=[dstid(hc)], dma_engine_mask=((1 << hop_ne) - 1) << (hop_ne * i),
+                                            remote_sem=hop[c], src=stage[d][s], dst=stage[d][s])
+                     for i, (d, s, hc) in enumerate(blk)],
+                    local_sem=S.sent)
+                sent += hop_ne * len(blk)
+            for rel, d in mine:
+                if c < CHUNKS[d]:
+                    if d not in have:
+                        g.wait_ge(ld[d][c], 16)
+                        have.add(d)
+                    sent += scatter(rel, d, c)
+    elif mine:
+        for c in range(maxc):
+            todo = [(rel, d) for rel, d in mine if c < CHUNKS[d]]
+            if todo:
+                g.wait_ge(hop[c], 8 * len(todo) * hop_ne)
+            for rel, d in todo:
+                sent += scatter(rel, d, c)
+
+    for d in (0, 1):
+        if k != OWNER[d]:
+            continue
+        m = comms_topo.mask(core, root)
+        for c in range(CHUNKS[d]):
+            g.wait_ge(arr[c], NCHIP)
+            g.remote_dma_fused(
+                [bass.RemoteDMATransfer(dst_ids=[dstid(root)], dma_engine_mask=m, remote_sem=fin[d][c],
+                                        srcs=[gat[d][c * NCHIP + sc] for sc in range(NCHIP)],
+                                        dsts=[land[d][c * NCHIP + ch]], alu_op=1)],
+                local_sem=S.sent)
+            sent += bin(m).count("1")
+
+    if core == root:
+        n = 0
+        for c in range(maxc):
+            for d in (0, 1):
+                if c < CHUNKS[d]:
+                    r0, r1 = xrows(d, c)
+                    g.wait_ge(fin[d][c], 15 * 8 + 16)
+                    g.dma_start(T.y[r0:r1, :], land[d][c * NCHIP:(c + 1) * NCHIP]).then_inc(S.st, 16)
+                    n += 16
+        g.wait_ge(S.st, n)
+
+    if sent:
+        g.wait_ge(S.sent, sent)

@@ -2,26 +2,19 @@ import concourse.bass as bass
 import comms_topo
 
 NCHIP = 16
+W = 32
 RANKCORE = 6
 ROOTRANK = 12
 OWNER = {0: 7, 1: 3}
-WIDTH = {0: 32, 1: 32}
-CHUNKS = {0: 1, 1: 1}
 SENDER = {("same", 0): 6, ("cross", 0): 6, ("cross", 1): 2, ("same", 1): 0}
 SEND_ORDER = [("cross", 1), ("same", 1), ("cross", 0), ("same", 0)]
 
 SCRATCH = {
-    "stage0": ("dram", [NCHIP * CHUNKS[0], 128, WIDTH[0]], "float32"),
-    "stage1": ("dram", [NCHIP * CHUNKS[1], 128, WIDTH[1]], "float32"),
-    "gat0": ("dram", [NCHIP * CHUNKS[0], 128, WIDTH[0]], "float32"),
-    "gat1": ("dram", [NCHIP * CHUNKS[1], 128, WIDTH[1]], "float32"),
-    "land0": ("dram", [NCHIP * CHUNKS[0], 128, WIDTH[0]], "float32"),
-    "land1": ("dram", [NCHIP * CHUNKS[1], 128, WIDTH[1]], "float32"),
+    "stage": ("dram", [2 * NCHIP, 128, W], "float32"),
+    "gat": ("dram", [NCHIP, 128, W], "float32"),
+    "land": ("dram", [2 * NCHIP, 128, W], "float32"),
 }
-SEMAPHORES = ["st", "sent",
-              "ld00", "ld01", "ld02", "ld03", "ld10", "ld11", "ld12", "ld13",
-              "hop0", "hop1", "hop2", "hop3", "arr0", "arr1", "arr2", "arr3",
-              "fin00", "fin01", "fin02", "fin03", "fin10", "fin11", "fin12", "fin13"]
+SEMAPHORES = ["ld0", "ld1", "st", "hop", "arr", "fin0", "fin1", "sent"]
 
 
 def dstid(c):
@@ -29,102 +22,65 @@ def dstid(c):
     return bass.DstId(rid=rid, pnc=pid)
 
 
-def chips_of(par):
-    return [c for c in range(NCHIP) if (c & 1) == par]
-
-
 def rank_program(g, core, T, topo):
     ch, k = divmod(core, 8)
     par = ch & 1
     root = T.cores[ROOTRANK]
     S = T.sem
-    stage = {0: T.stage0, 1: T.stage1}
-    gat = {0: T.gat0, 1: T.gat1}
-    land = {0: T.land0, 1: T.land1}
-    ld = {0: [S.ld00, S.ld01, S.ld02, S.ld03], 1: [S.ld10, S.ld11, S.ld12, S.ld13]}
-    fin = {0: [S.fin00, S.fin01, S.fin02, S.fin03], 1: [S.fin10, S.fin11, S.fin12, S.fin13]}
-    hop = [S.hop0, S.hop1, S.hop2, S.hop3]
-    arr = [S.arr0, S.arr1, S.arr2, S.arr3]
-    maxc = max(CHUNKS.values())
+    fin = {0: S.fin0, 1: S.fin1}
     sent = 0
 
-    def xrows(d, c):
-        r0 = (0 if d == 0 else 2 * WIDTH[0] * CHUNKS[0]) + 2 * WIDTH[d] * c
-        return r0, r0 + 2 * WIDTH[d]
+    def owners(rel):
+        p = par if rel == "same" else 1 - par
+        return [c for c in range(NCHIP) if (c & 1) == p]
 
-    def owner_par(rel):
-        return par if rel == "same" else 1 - par
-
-    def scatter(rel, d, c):
-        trs = [bass.RemoteDMATransfer(dst_ids=[dstid(oc * 8 + OWNER[d])], dma_engine_mask=1 << i,
-                                      remote_sem=arr[c], src=stage[d][c * NCHIP + oc], dst=gat[d][c * NCHIP + ch])
-               for i, oc in enumerate(chips_of(owner_par(rel)))]
-        g.remote_dma_fused(trs, local_sem=S.sent)
-        return len(trs)
+    def scatter(rel, d):
+        g.remote_dma_fused(
+            [bass.RemoteDMATransfer(dst_ids=[dstid(oc * 8 + OWNER[d])], dma_engine_mask=1 << i,
+                                    remote_sem=S.arr, src=T.stage[d * NCHIP + oc], dst=T.gat[ch])
+             for i, oc in enumerate(owners(rel))],
+            local_sem=S.sent)
+        return 8
 
     hops = [key for key in SEND_ORDER if SENDER[key] != RANKCORE]
     mine = [key for key in SEND_ORDER if SENDER[key] == k]
-    hop_ne = 16 // (8 * len(hops)) if len(hops) in (1, 2) else 1
 
     if k == RANKCORE:
-        for c in range(maxc):
-            for d in (1, 0):
-                if c < CHUNKS[d]:
-                    r0, r1 = xrows(d, c)
-                    g.dma_start(stage[d][c * NCHIP:(c + 1) * NCHIP], T.x[r0:r1, :]).then_inc(ld[d][c], 16)
-        for c in range(maxc):
-            have = set()
-            trs = [(d, c * NCHIP + oc, ch * 8 + SENDER[(rel, d)])
-                   for rel, d in hops if c < CHUNKS[d] for oc in chips_of(owner_par(rel))]
-            for d in (1, 0):
-                if any(t[0] == d for t in trs):
-                    g.wait_ge(ld[d][c], 16)
-                    have.add(d)
-            for i0 in range(0, len(trs), 16):
-                blk = trs[i0:i0 + 16]
-                g.remote_dma_fused(
-                    [bass.RemoteDMATransfer(dst_ids=[dstid(hc)], dma_engine_mask=((1 << hop_ne) - 1) << (hop_ne * i),
-                                            remote_sem=hop[c], src=stage[d][s], dst=stage[d][s])
-                     for i, (d, s, hc) in enumerate(blk)],
-                    local_sem=S.sent)
-                sent += hop_ne * len(blk)
-            for rel, d in mine:
-                if c < CHUNKS[d]:
-                    if d not in have:
-                        g.wait_ge(ld[d][c], 16)
-                        have.add(d)
-                    sent += scatter(rel, d, c)
+        g.dma_start(T.stage[NCHIP:2 * NCHIP], T.x[64:128, :]).then_inc(S.ld1, 16)
+        g.dma_start(T.stage[0:NCHIP], T.x[0:64, :]).then_inc(S.ld0, 16)
+        g.wait_ge(S.ld1, 16)
+        trs = [(d * NCHIP + oc, ch * 8 + SENDER[(rel, d)]) for rel, d in hops for oc in owners(rel)]
+        g.remote_dma_fused(
+            [bass.RemoteDMATransfer(dst_ids=[dstid(hc)], dma_engine_mask=1 << i,
+                                    remote_sem=S.hop, src=T.stage[s], dst=T.stage[s])
+             for i, (s, hc) in enumerate(trs)],
+            local_sem=S.sent)
+        sent += len(trs)
+        g.wait_ge(S.ld0, 16)
+        for rel, d in mine:
+            sent += scatter(rel, d)
     elif mine:
-        for c in range(maxc):
-            todo = [(rel, d) for rel, d in mine if c < CHUNKS[d]]
-            if todo:
-                g.wait_ge(hop[c], 8 * len(todo) * hop_ne)
-            for rel, d in todo:
-                sent += scatter(rel, d, c)
+        g.wait_ge(S.hop, 8 * len(mine))
+        for rel, d in mine:
+            sent += scatter(rel, d)
 
     for d in (0, 1):
-        if k != OWNER[d]:
-            continue
-        m = comms_topo.mask(core, root)
-        for c in range(CHUNKS[d]):
-            g.wait_ge(arr[c], NCHIP)
+        if k == OWNER[d]:
+            m = comms_topo.mask(core, root)
+            g.wait_ge(S.arr, NCHIP)
             g.remote_dma_fused(
-                [bass.RemoteDMATransfer(dst_ids=[dstid(root)], dma_engine_mask=m, remote_sem=fin[d][c],
-                                        srcs=[gat[d][c * NCHIP + sc] for sc in range(NCHIP)],
-                                        dsts=[land[d][c * NCHIP + ch]], alu_op=1)],
+                [bass.RemoteDMATransfer(dst_ids=[dstid(root)], dma_engine_mask=m, remote_sem=fin[d],
+                                        srcs=[T.gat[sc] for sc in range(NCHIP)],
+                                        dsts=[T.land[d * NCHIP + ch]], alu_op=1)],
                 local_sem=S.sent)
             sent += bin(m).count("1")
 
     if core == root:
-        n = 0
-        for c in range(maxc):
-            for d in (0, 1):
-                if c < CHUNKS[d]:
-                    r0, r1 = xrows(d, c)
-                    g.wait_ge(fin[d][c], 15 * 8 + 16)
-                    g.dma_start(T.y[r0:r1, :], land[d][c * NCHIP:(c + 1) * NCHIP]).then_inc(S.st, 16)
-                    n += 16
-        g.wait_ge(S.st, n)
+        g.wait_ge(S.fin0, 15 * 8 + 16)
+        g.dma_start(T.y[0:64, :], T.land[0:NCHIP]).then_inc(S.st, 16)
+        g.wait_ge(S.fin1, 15 * 8 + 16)
+        g.dma_start(T.y[64:128, :], T.land[NCHIP:2 * NCHIP]).then_inc(S.st, 16)
+        g.wait_ge(S.st, 32)
 
     if sent:
         g.wait_ge(S.sent, sent)

import concourse.bass as bass
import comms_topo

NCHIP = 16
W = 32
RANKCORE = 6
ROOTRANK = 12
OWNER = {0: 7, 1: 3}
SENDER = {("same", 0): 6, ("cross", 0): 6, ("cross", 1): 2, ("same", 1): 0}
SEND_ORDER = [("cross", 1), ("same", 1), ("cross", 0), ("same", 0)]

SCRATCH = {
    "stage": ("dram", [2 * NCHIP, 128, W], "float32"),
    "gat": ("dram", [NCHIP, 128, W], "float32"),
    "land": ("dram", [2 * NCHIP, 128, W], "float32"),
}
SEMAPHORES = ["ld0", "ld1", "st", "hop", "arr", "fin0", "fin1", "sent"]


def dstid(c):
    rid, pid, se = comms_topo.addr(c)
    return bass.DstId(rid=rid, pnc=pid)


def rank_program(g, core, T, topo):
    ch, k = divmod(core, 8)
    par = ch & 1
    root = T.cores[ROOTRANK]
    S = T.sem
    fin = {0: S.fin0, 1: S.fin1}
    sent = 0

    def owners(rel):
        p = par if rel == "same" else 1 - par
        return [c for c in range(NCHIP) if (c & 1) == p]

    def scatter(rel, d):
        g.remote_dma_fused(
            [bass.RemoteDMATransfer(dst_ids=[dstid(oc * 8 + OWNER[d])], dma_engine_mask=1 << i,
                                    remote_sem=S.arr, src=T.stage[d * NCHIP + oc], dst=T.gat[ch])
             for i, oc in enumerate(owners(rel))],
            local_sem=S.sent)
        return 8

    hops = [key for key in SEND_ORDER if SENDER[key] != RANKCORE]
    mine = [key for key in SEND_ORDER if SENDER[key] == k]

    if k == RANKCORE:
        g.dma_start(T.stage[NCHIP:2 * NCHIP], T.x[64:128, :]).then_inc(S.ld1, 16)
        g.dma_start(T.stage[0:NCHIP], T.x[0:64, :]).then_inc(S.ld0, 16)
        g.wait_ge(S.ld1, 16)
        trs = [(d * NCHIP + oc, ch * 8 + SENDER[(rel, d)]) for rel, d in hops for oc in owners(rel)]
        g.remote_dma_fused(
            [bass.RemoteDMATransfer(dst_ids=[dstid(hc)], dma_engine_mask=1 << i,
                                    remote_sem=S.hop, src=T.stage[s], dst=T.stage[s])
             for i, (s, hc) in enumerate(trs)],
            local_sem=S.sent)
        sent += len(trs)
        g.wait_ge(S.ld0, 16)
        for rel, d in mine:
            sent += scatter(rel, d)
    elif mine:
        g.wait_ge(S.hop, 8 * len(mine))
        for rel, d in mine:
            sent += scatter(rel, d)

    for d in (0, 1):
        if k == OWNER[d]:
            m = comms_topo.mask(core, root)
            g.wait_ge(S.arr, NCHIP)
            g.remote_dma_fused(
                [bass.RemoteDMATransfer(dst_ids=[dstid(root)], dma_engine_mask=m, remote_sem=fin[d],
                                        srcs=[T.gat[sc] for sc in range(NCHIP)],
                                        dsts=[T.land[d * NCHIP + ch]], alu_op=1)],
                local_sem=S.sent)
            sent += bin(m).count("1")

    if core == root:
        g.wait_ge(S.fin0, 15 * 8 + 16)
        g.dma_start(T.y[0:64, :], T.land[0:NCHIP]).then_inc(S.st, 16)
        g.wait_ge(S.fin1, 15 * 8 + 16)
        g.dma_start(T.y[64:128, :], T.land[NCHIP:2 * NCHIP]).then_inc(S.st, 16)
        g.wait_ge(S.st, 32)

    if sent:
        g.wait_ge(S.sent, sent)
